import numpy as np
CORES = [0,1,2,3,4,5,6,7,24,25,26,27,28,29,30,31]
N = 16
def setup_inputs(rng):
    return {"x": rng.standard_normal((N, 128, 4096), dtype=np.float32)}
def reference(x):
    s = x.sum(axis=0, dtype=np.float64).astype(x.dtype)
    b = 4096 // N
    return {"y": np.stack([s[:, r * b:(r + 1) * b] for r in range(N)])}

@@ -1,0 +1,150 @@
+import concourse.bass as bass
+import concourse.mybir as mybir
+
+B = 256
+FINAL = "LC"
+SPLIT = False
+LF_MASK = 0xFFFF
+FCH = 1
+
+SCRATCH = {
+    "xs": ("sbuf", [128, 16 * B], "float32"),
+    "la": ("sbuf", [128, 7 * B], "float32"),
+    "lb": ("sbuf", [128, 7 * B], "float32"),
+    "fw": ("sbuf", [128, B], "float32"),
+    "cp": ("sbuf", [128, B], "float32"),
+    "lp": ("sbuf", [128, B], "float32"),
+}
+SEMAPHORES = ["ld0", "ld1", "ld2", "ld3", "arrA", "arrB", "arrF0", "arrF1", "arrF2", "arrF3", "arrC", "arrL", "sent",
+              "st1", "st2"]
+
+GATE = (2, 3, 6, 7)
+A_FOLDER = (0, 1, 4, 5, 2, 3, 6, 7) if SPLIT else (0, 1, 2, 3, 4, 5, 6, 7)
+
+
+def blk(t, j):
+    return t[:, j * B:(j + 1) * B]
+
+
+def piece(t, j, p):
+    w = B // FCH
+    return t[:, j * B + p * w:j * B + (p + 1) * w]
+
+
+def rank_program(g, core, T, topo):
+    ch, k = divmod(core, 8)
+    S = T.sem
+    arrF = [S.arrF0, S.arrF1, S.arrF2, S.arrF3]
+
+    def dst_id(c):
+        rid, pid, se = topo.addr(c)
+        return bass.DstId(rid=rid, pnc=pid)
+
+    def c_home(j):
+        return j ^ 1 if FINAL == "F9" else j
+
+    if ch in (1, 2):
+        if k not in GATE:
+            return
+        j = A_FOLDER.index(k - 2)
+        rid, pid, se = topo.addr((24 if ch == 2 else 0) + c_home(j))
+        for p in range(FCH):
+            g.wait_ge(arrF[p], 8)
+            g.remote_dma(out_ap=piece(T.cp, 0, p), in_ap=piece(T.fw, 0, p), remote_sem=S.arrC, local_sem=S.sent,
+                         pid=pid, routing_id=rid, dma_engine_mask=0xFF)
+        g.wait_ge(S.sent, 8 * FCH)
+        return
+
+    base = ch * 8
+    other = 24 - base
+    helper = 16 if ch == 0 else 8
+    loc0 = 0 if ch == 0 else 8
+    rem0 = 8 - loc0
+
+    a = [(rem0 + j, A_FOLDER[j]) for j in range(8)]
+    b = [(loc0 + j, j ^ 1) for j in range(8)]
+    if SPLIT:
+        groups = [(a[:4], T.la, S.arrA), (a[4:], T.la, S.arrA), (b[:4], T.lb, S.arrB), (b[4:], T.lb, S.arrB)]
+    else:
+        groups = [(a, T.la, S.arrA), (b, T.lb, S.arrB)]
+    lds = [S.ld0, S.ld1, S.ld2, S.ld3]
+    eng = 16 // len(groups[0][0])
+    sent = [0]
+
+    def load(i):
+        c0 = groups[i][0][0][0] * B
+        c1 = (groups[i][0][-1][0] + 1) * B
+        g.dma_start(out=T.xs[:, c0:c1], in_=T.x[:, c0:c1]).then_inc(lds[i], 16)
+
+    def fold_a():
+        ja = A_FOLDER.index(k)
+        g.wait_ge(S.arrA, 7 * eng)
+        if k in GATE:
+            srcs = [blk(T.la, s) for s in range(7)] + [blk(T.xs, rem0 + ja)]
+            tr = bass.RemoteDMATransfer(dst_ids=[dst_id(other + c_home(ja))], dma_engine_mask=0xFF,
+                                        remote_sem=S.arrC, srcs=srcs, dsts=[T.cp[:]], alu_op=1)
+            g.remote_dma_fused([tr], local_sem=S.sent)
+            sent[0] += 8
+        else:
+            for p in range(FCH):
+                srcs = [piece(T.la, s, p) for s in range(7)] + [piece(T.xs, rem0 + ja, p)]
+                tr = bass.RemoteDMATransfer(dst_ids=[dst_id(helper + k + 2)], dma_engine_mask=0xFF,
+                                            remote_sem=arrF[p], srcs=srcs, dsts=[piece(T.fw, 0, p)], alu_op=1)
+                g.remote_dma_fused([tr], local_sem=S.sent)
+                sent[0] += 8
+
+    load(0)
+    load(1)
+    for i, (blocks, land, sem) in enumerate(groups):
+        if SPLIT and i == 3 and k not in GATE:
+            fold_a()
+        g.wait_ge(lds[i], 16)
+        trs = []
+        for pos, (bj, m) in enumerate(blocks):
+            if m == k:
+                continue
+            slot = k if k < m else k - 1
+            trs.append(bass.RemoteDMATransfer(dst_ids=[dst_id(base + m)],
+                                              dma_engine_mask=((1 << eng) - 1) << (eng * pos),
+                                              remote_sem=sem, src=blk(T.xs, bj), dst=blk(land, slot)))
+        g.remote_dma_fused(trs, local_sem=S.sent)
+        sent[0] += eng * len(trs)
+        if i + 2 < len(groups):
+            load(i + 2)
+    if not (SPLIT and k not in GATE):
+        fold_a()
+
+    jc = c_home(k)
+    n_c = 8 if A_FOLDER[jc] in GATE else 8 * FCH
+
+    nl = bin(LF_MASK).count("1")
+    g.wait_ge(S.arrB, 7 * eng)
+    srcs = [blk(T.lb, s) for s in range(7)] + [blk(T.xs, loc0 + (k ^ 1))]
+    if FINAL == "F9":
+        g.wait_ge(S.arrC, n_c)
+        srcs.append(T.cp[:])
+    g.remote_dma_fused([bass.RemoteDMATransfer(dst_ids=[dst_id(base + (k ^ 1))], dma_engine_mask=LF_MASK,
+                                               remote_sem=S.arrL, srcs=srcs, dsts=[T.lp[:]], alu_op=1)],
+                       local_sem=S.sent)
+    sent[0] += nl
+
+    add = mybir.AluOpType.add
+    if FINAL == "F9":
+        g.wait_ge(S.arrL, nl)
+        g.dma_start(out=T.y[:], in_=T.lp[:]).then_inc(S.st1, 16)
+        g.wait_ge(S.st1, 16)
+    elif FINAL == "LC":
+        g.wait_ge(S.arrL, nl)
+        g.dma_start(out=T.y[:], in_=T.lp[:]).then_inc(S.st1, 16)
+        g.wait_ge(S.st1, 16)
+        g.wait_ge(S.arrC, n_c)
+        g.dma_start(out=T.y[:], in_=T.cp[:], accum_op=add).then_inc(S.st2, 16)
+        g.wait_ge(S.st2, 16)
+    else:
+        g.wait_ge(S.arrC, n_c)
+        g.dma_start(out=T.y[:], in_=T.cp[:]).then_inc(S.st1, 16)
+        g.wait_ge(S.st1, 16)
+        g.wait_ge(S.arrL, nl)
+        g.dma_start(out=T.y[:], in_=T.lp[:], accum_op=add).then_inc(S.st2, 16)
+        g.wait_ge(S.st2, 16)
+    g.wait_ge(S.sent, sent[0])

@@ -2,10 +2,7 @@ import concourse.bass as bass
 import concourse.mybir as mybir
 
 B = 256
-FINAL = "LC"
-SPLIT = False
-LF_MASK = 0xFFFF
-FCH = 1
+LF_MASK = 0xFF00
 
 SCRATCH = {
     "xs": ("sbuf", [128, 16 * B], "float32"),
@@ -15,44 +12,31 @@ SCRATCH = {
     "cp": ("sbuf", [128, B], "float32"),
     "lp": ("sbuf", [128, B], "float32"),
 }
-SEMAPHORES = ["ld0", "ld1", "ld2", "ld3", "arrA", "arrB", "arrF0", "arrF1", "arrF2", "arrF3", "arrC", "arrL", "sent",
-              "st1", "st2"]
+SEMAPHORES = ["ld0", "ld1", "arrA", "arrB", "arrF", "arrC", "arrL", "sent", "st1", "st2"]
 
 GATE = (2, 3, 6, 7)
-A_FOLDER = (0, 1, 4, 5, 2, 3, 6, 7) if SPLIT else (0, 1, 2, 3, 4, 5, 6, 7)
 
 
 def blk(t, j):
     return t[:, j * B:(j + 1) * B]
 
 
-def piece(t, j, p):
-    w = B // FCH
-    return t[:, j * B + p * w:j * B + (p + 1) * w]
-
-
 def rank_program(g, core, T, topo):
     ch, k = divmod(core, 8)
     S = T.sem
-    arrF = [S.arrF0, S.arrF1, S.arrF2, S.arrF3]
 
     def dst_id(c):
         rid, pid, se = topo.addr(c)
         return bass.DstId(rid=rid, pnc=pid)
 
-    def c_home(j):
-        return j ^ 1 if FINAL == "F9" else j
-
     if ch in (1, 2):
         if k not in GATE:
             return
-        j = A_FOLDER.index(k - 2)
-        rid, pid, se = topo.addr((24 if ch == 2 else 0) + c_home(j))
-        for p in range(FCH):
-            g.wait_ge(arrF[p], 8)
-            g.remote_dma(out_ap=piece(T.cp, 0, p), in_ap=piece(T.fw, 0, p), remote_sem=S.arrC, local_sem=S.sent,
-                         pid=pid, routing_id=rid, dma_engine_mask=0xFF)
-        g.wait_ge(S.sent, 8 * FCH)
+        rid, pid, se = topo.addr((24 if ch == 2 else 0) + k - 2)
+        g.wait_ge(S.arrF, 8)
+        g.remote_dma(out_ap=T.cp[:], in_ap=T.fw[:], remote_sem=S.arrC, local_sem=S.sent, pid=pid, routing_id=rid,
+                     dma_engine_mask=0xFF)
+        g.wait_ge(S.sent, 8)
         return
 
     base = ch * 8
@@ -60,91 +44,46 @@ def rank_program(g, core, T, topo):
     helper = 16 if ch == 0 else 8
     loc0 = 0 if ch == 0 else 8
     rem0 = 8 - loc0
+    sent = 0
 
-    a = [(rem0 + j, A_FOLDER[j]) for j in range(8)]
-    b = [(loc0 + j, j ^ 1) for j in range(8)]
-    if SPLIT:
-        groups = [(a[:4], T.la, S.arrA), (a[4:], T.la, S.arrA), (b[:4], T.lb, S.arrB), (b[4:], T.lb, S.arrB)]
-    else:
-        groups = [(a, T.la, S.arrA), (b, T.lb, S.arrB)]
-    lds = [S.ld0, S.ld1, S.ld2, S.ld3]
-    eng = 16 // len(groups[0][0])
-    sent = [0]
-
-    def load(i):
-        c0 = groups[i][0][0][0] * B
-        c1 = (groups[i][0][-1][0] + 1) * B
-        g.dma_start(out=T.xs[:, c0:c1], in_=T.x[:, c0:c1]).then_inc(lds[i], 16)
-
-    def fold_a():
-        ja = A_FOLDER.index(k)
-        g.wait_ge(S.arrA, 7 * eng)
-        if k in GATE:
-            srcs = [blk(T.la, s) for s in range(7)] + [blk(T.xs, rem0 + ja)]
-            tr = bass.RemoteDMATransfer(dst_ids=[dst_id(other + c_home(ja))], dma_engine_mask=0xFF,
-                                        remote_sem=S.arrC, srcs=srcs, dsts=[T.cp[:]], alu_op=1)
-            g.remote_dma_fused([tr], local_sem=S.sent)
-            sent[0] += 8
-        else:
-            for p in range(FCH):
-                srcs = [piece(T.la, s, p) for s in range(7)] + [piece(T.xs, rem0 + ja, p)]
-                tr = bass.RemoteDMATransfer(dst_ids=[dst_id(helper + k + 2)], dma_engine_mask=0xFF,
-                                            remote_sem=arrF[p], srcs=srcs, dsts=[piece(T.fw, 0, p)], alu_op=1)
-                g.remote_dma_fused([tr], local_sem=S.sent)
-                sent[0] += 8
-
-    load(0)
-    load(1)
-    for i, (blocks, land, sem) in enumerate(groups):
-        if SPLIT and i == 3 and k not in GATE:
-            fold_a()
-        g.wait_ge(lds[i], 16)
+    halves = [(rem0, 0, T.la, S.arrA, S.ld0), (loc0, 1, T.lb, S.arrB, S.ld1)]
+    for b0, flip, land, sem, ld in halves:
+        g.dma_start(out=T.xs[:, b0 * B:(b0 + 8) * B], in_=T.x[:, b0 * B:(b0 + 8) * B]).then_inc(ld, 16)
+    for b0, flip, land, sem, ld in halves:
+        g.wait_ge(ld, 16)
         trs = []
-        for pos, (bj, m) in enumerate(blocks):
+        for j in range(8):
+            m = j ^ flip
             if m == k:
                 continue
             slot = k if k < m else k - 1
-            trs.append(bass.RemoteDMATransfer(dst_ids=[dst_id(base + m)],
-                                              dma_engine_mask=((1 << eng) - 1) << (eng * pos),
-                                              remote_sem=sem, src=blk(T.xs, bj), dst=blk(land, slot)))
+            trs.append(bass.RemoteDMATransfer(dst_ids=[dst_id(base + m)], dma_engine_mask=0x3 << (2 * len(trs)),
+                                              remote_sem=sem, src=blk(T.xs, b0 + j), dst=blk(land, slot)))
         g.remote_dma_fused(trs, local_sem=S.sent)
-        sent[0] += eng * len(trs)
-        if i + 2 < len(groups):
-            load(i + 2)
-    if not (SPLIT and k not in GATE):
-        fold_a()
+        sent += 14
 
-    jc = c_home(k)
-    n_c = 8 if A_FOLDER[jc] in GATE else 8 * FCH
+    g.wait_ge(S.arrA, 14)
+    srcs = [blk(T.la, s) for s in range(7)] + [blk(T.xs, rem0 + k)]
+    if k in GATE:
+        tr = bass.RemoteDMATransfer(dst_ids=[dst_id(other + k)], dma_engine_mask=0xFF,
+                                    remote_sem=S.arrC, srcs=srcs, dsts=[T.cp[:]], alu_op=1)
+    else:
+        tr = bass.RemoteDMATransfer(dst_ids=[dst_id(helper + k + 2)], dma_engine_mask=0xFF,
+                                    remote_sem=S.arrF, srcs=srcs, dsts=[T.fw[:]], alu_op=1)
+    g.remote_dma_fused([tr], local_sem=S.sent)
+    sent += 8
 
-    nl = bin(LF_MASK).count("1")
-    g.wait_ge(S.arrB, 7 * eng)
+    g.wait_ge(S.arrB, 14)
     srcs = [blk(T.lb, s) for s in range(7)] + [blk(T.xs, loc0 + (k ^ 1))]
-    if FINAL == "F9":
-        g.wait_ge(S.arrC, n_c)
-        srcs.append(T.cp[:])
     g.remote_dma_fused([bass.RemoteDMATransfer(dst_ids=[dst_id(base + (k ^ 1))], dma_engine_mask=LF_MASK,
                                                remote_sem=S.arrL, srcs=srcs, dsts=[T.lp[:]], alu_op=1)],
                        local_sem=S.sent)
-    sent[0] += nl
+    sent += 8
 
-    add = mybir.AluOpType.add
-    if FINAL == "F9":
-        g.wait_ge(S.arrL, nl)
-        g.dma_start(out=T.y[:], in_=T.lp[:]).then_inc(S.st1, 16)
-        g.wait_ge(S.st1, 16)
-    elif FINAL == "LC":
-        g.wait_ge(S.arrL, nl)
-        g.dma_start(out=T.y[:], in_=T.lp[:]).then_inc(S.st1, 16)
-        g.wait_ge(S.st1, 16)
-        g.wait_ge(S.arrC, n_c)
-        g.dma_start(out=T.y[:], in_=T.cp[:], accum_op=add).then_inc(S.st2, 16)
-        g.wait_ge(S.st2, 16)
-    else:
-        g.wait_ge(S.arrC, n_c)
-        g.dma_start(out=T.y[:], in_=T.cp[:]).then_inc(S.st1, 16)
-        g.wait_ge(S.st1, 16)
-        g.wait_ge(S.arrL, nl)
-        g.dma_start(out=T.y[:], in_=T.lp[:], accum_op=add).then_inc(S.st2, 16)
-        g.wait_ge(S.st2, 16)
-    g.wait_ge(S.sent, sent[0])
+    g.wait_ge(S.arrL, 8)
+    g.dma_start(out=T.y[:], in_=T.lp[:]).then_inc(S.st1, 16)
+    g.wait_ge(S.st1, 16)
+    g.wait_ge(S.arrC, 8)
+    g.dma_start(out=T.y[:], in_=T.cp[:], accum_op=mybir.AluOpType.add).then_inc(S.st2, 16)
+    g.wait_ge(S.st2, 16)
+    g.wait_ge(S.sent, sent)

@@ -3,6 +3,7 @@ import concourse.mybir as mybir
 
 B = 256
 LF_MASK = 0xFF00
+FCH = 2
 
 SCRATCH = {
     "xs": ("sbuf", [128, 16 * B], "float32"),
@@ -12,7 +13,7 @@ SCRATCH = {
     "cp": ("sbuf", [128, B], "float32"),
     "lp": ("sbuf", [128, B], "float32"),
 }
-SEMAPHORES = ["ld0", "ld1", "arrA", "arrB", "arrF", "arrC", "arrL", "sent", "st1", "st2"]
+SEMAPHORES = ["ld0", "ld1", "arrA", "arrB", "arrF0", "arrF1", "arrF2", "arrF3", "arrC", "arrL", "sent", "st1", "st2"]
 
 GATE = (2, 3, 6, 7)
 
@@ -21,9 +22,15 @@ def blk(t, j):
     return t[:, j * B:(j + 1) * B]
 
 
+def piece(t, j, p):
+    w = B // FCH
+    return t[:, j * B + p * w:j * B + (p + 1) * w]
+
+
 def rank_program(g, core, T, topo):
     ch, k = divmod(core, 8)
     S = T.sem
+    arrF = [S.arrF0, S.arrF1, S.arrF2, S.arrF3]
 
     def dst_id(c):
         rid, pid, se = topo.addr(c)
@@ -33,10 +40,11 @@ def rank_program(g, core, T, topo):
         if k not in GATE:
             return
         rid, pid, se = topo.addr((24 if ch == 2 else 0) + k - 2)
-        g.wait_ge(S.arrF, 8)
-        g.remote_dma(out_ap=T.cp[:], in_ap=T.fw[:], remote_sem=S.arrC, local_sem=S.sent, pid=pid, routing_id=rid,
-                     dma_engine_mask=0xFF)
-        g.wait_ge(S.sent, 8)
+        for p in range(FCH):
+            g.wait_ge(arrF[p], 8)
+            g.remote_dma(out_ap=piece(T.cp, 0, p), in_ap=piece(T.fw, 0, p), remote_sem=S.arrC, local_sem=S.sent,
+                         pid=pid, routing_id=rid, dma_engine_mask=0xFF)
+        g.wait_ge(S.sent, 8 * FCH)
         return
 
     base = ch * 8
@@ -63,15 +71,19 @@ def rank_program(g, core, T, topo):
         sent += 14
 
     g.wait_ge(S.arrA, 14)
-    srcs = [blk(T.la, s) for s in range(7)] + [blk(T.xs, rem0 + k)]
     if k in GATE:
+        srcs = [blk(T.la, s) for s in range(7)] + [blk(T.xs, rem0 + k)]
         tr = bass.RemoteDMATransfer(dst_ids=[dst_id(other + k)], dma_engine_mask=0xFF,
                                     remote_sem=S.arrC, srcs=srcs, dsts=[T.cp[:]], alu_op=1)
+        g.remote_dma_fused([tr], local_sem=S.sent)
+        sent += 8
     else:
-        tr = bass.RemoteDMATransfer(dst_ids=[dst_id(helper + k + 2)], dma_engine_mask=0xFF,
-                                    remote_sem=S.arrF, srcs=srcs, dsts=[T.fw[:]], alu_op=1)
-    g.remote_dma_fused([tr], local_sem=S.sent)
-    sent += 8
+        for p in range(FCH):
+            srcs = [piece(T.la, s, p) for s in range(7)] + [piece(T.xs, rem0 + k, p)]
+            tr = bass.RemoteDMATransfer(dst_ids=[dst_id(helper + k + 2)], dma_engine_mask=0xFF,
+                                        remote_sem=arrF[p], srcs=srcs, dsts=[piece(T.fw, 0, p)], alu_op=1)
+            g.remote_dma_fused([tr], local_sem=S.sent)
+            sent += 8
 
     g.wait_ge(S.arrB, 14)
     srcs = [blk(T.lb, s) for s in range(7)] + [blk(T.xs, loc0 + (k ^ 1))]
@@ -83,7 +95,7 @@ def rank_program(g, core, T, topo):
     g.wait_ge(S.arrL, 8)
     g.dma_start(out=T.y[:], in_=T.lp[:]).then_inc(S.st1, 16)
     g.wait_ge(S.st1, 16)
-    g.wait_ge(S.arrC, 8)
+    g.wait_ge(S.arrC, 8 if k in GATE else 8 * FCH)
     g.dma_start(out=T.y[:], in_=T.cp[:], accum_op=mybir.AluOpType.add).then_inc(S.st2, 16)
     g.wait_ge(S.st2, 16)
     g.wait_ge(S.sent, sent)

import concourse.bass as bass
import concourse.mybir as mybir

B = 256
LF_MASK = 0xFF00
FCH = 2

SCRATCH = {
    "xs": ("sbuf", [128, 16 * B], "float32"),
    "la": ("sbuf", [128, 7 * B], "float32"),
    "lb": ("sbuf", [128, 7 * B], "float32"),
    "fw": ("sbuf", [128, B], "float32"),
    "cp": ("sbuf", [128, B], "float32"),
    "lp": ("sbuf", [128, B], "float32"),
}
SEMAPHORES = ["ld0", "ld1", "arrA", "arrB", "arrF0", "arrF1", "arrF2", "arrF3", "arrC", "arrL", "sent", "st1", "st2"]

GATE = (2, 3, 6, 7)


def blk(t, j):
    return t[:, j * B:(j + 1) * B]


def piece(t, j, p):
    w = B // FCH
    return t[:, j * B + p * w:j * B + (p + 1) * w]


def rank_program(g, core, T, topo):
    ch, k = divmod(core, 8)
    S = T.sem
    arrF = [S.arrF0, S.arrF1, S.arrF2, S.arrF3]

    def dst_id(c):
        rid, pid, se = topo.addr(c)
        return bass.DstId(rid=rid, pnc=pid)

    if ch in (1, 2):
        if k not in GATE:
            return
        rid, pid, se = topo.addr((24 if ch == 2 else 0) + k - 2)
        for p in range(FCH):
            g.wait_ge(arrF[p], 8)
            g.remote_dma(out_ap=piece(T.cp, 0, p), in_ap=piece(T.fw, 0, p), remote_sem=S.arrC, local_sem=S.sent,
                         pid=pid, routing_id=rid, dma_engine_mask=0xFF)
        g.wait_ge(S.sent, 8 * FCH)
        return

    base = ch * 8
    other = 24 - base
    helper = 16 if ch == 0 else 8
    loc0 = 0 if ch == 0 else 8
    rem0 = 8 - loc0
    sent = 0

    halves = [(rem0, 0, T.la, S.arrA, S.ld0), (loc0, 1, T.lb, S.arrB, S.ld1)]
    for b0, flip, land, sem, ld in halves:
        g.dma_start(out=T.xs[:, b0 * B:(b0 + 8) * B], in_=T.x[:, b0 * B:(b0 + 8) * B]).then_inc(ld, 16)
    for b0, flip, land, sem, ld in halves:
        g.wait_ge(ld, 16)
        trs = []
        for j in range(8):
            m = j ^ flip
            if m == k:
                continue
            slot = k if k < m else k - 1
            trs.append(bass.RemoteDMATransfer(dst_ids=[dst_id(base + m)], dma_engine_mask=0x3 << (2 * len(trs)),
                                              remote_sem=sem, src=blk(T.xs, b0 + j), dst=blk(land, slot)))
        g.remote_dma_fused(trs, local_sem=S.sent)
        sent += 14

    g.wait_ge(S.arrA, 14)
    if k in GATE:
        srcs = [blk(T.la, s) for s in range(7)] + [blk(T.xs, rem0 + k)]
        tr = bass.RemoteDMATransfer(dst_ids=[dst_id(other + k)], dma_engine_mask=0xFF,
                                    remote_sem=S.arrC, srcs=srcs, dsts=[T.cp[:]], alu_op=1)
        g.remote_dma_fused([tr], local_sem=S.sent)
        sent += 8
    else:
        for p in range(FCH):
            srcs = [piece(T.la, s, p) for s in range(7)] + [piece(T.xs, rem0 + k, p)]
            tr = bass.RemoteDMATransfer(dst_ids=[dst_id(helper + k + 2)], dma_engine_mask=0xFF,
                                        remote_sem=arrF[p], srcs=srcs, dsts=[piece(T.fw, 0, p)], alu_op=1)
            g.remote_dma_fused([tr], local_sem=S.sent)
            sent += 8

    g.wait_ge(S.arrB, 14)
    srcs = [blk(T.lb, s) for s in range(7)] + [blk(T.xs, loc0 + (k ^ 1))]
    g.remote_dma_fused([bass.RemoteDMATransfer(dst_ids=[dst_id(base + (k ^ 1))], dma_engine_mask=LF_MASK,
                                               remote_sem=S.arrL, srcs=srcs, dsts=[T.lp[:]], alu_op=1)],
                       local_sem=S.sent)
    sent += 8

    g.wait_ge(S.arrL, 8)
    g.dma_start(out=T.y[:], in_=T.lp[:]).then_inc(S.st1, 16)
    g.wait_ge(S.st1, 16)
    g.wait_ge(S.arrC, 8 if k in GATE else 8 * FCH)
    g.dma_start(out=T.y[:], in_=T.cp[:], accum_op=mybir.AluOpType.add).then_inc(S.st2, 16)
    g.wait_ge(S.st2, 16)
    g.wait_ge(S.sent, sent)
